import numpy as np
import ml_dtypes


def mxq(x, axis, fmt="e4m3"):
    dtype, down = {"e4m3": (ml_dtypes.float8_e4m3fn, 7), "e5m2": (ml_dtypes.float8_e5m2, 14)}[fmt]
    v = np.moveaxis(np.asarray(x, np.float32).astype(ml_dtypes.bfloat16).astype(np.float64), axis, -1)
    blocks = v.reshape(v.shape[:-1] + (-1, 32))
    amax = np.abs(blocks).max(-1, keepdims=True)
    byte = np.maximum(np.where(amax > 0, np.frexp(amax)[1] - 1 + 127, 0) - down, 1)
    scale = np.exp2(byte - 127.0)
    codes = (blocks / scale).astype(np.float32).astype(dtype).astype(np.float64)
    return np.moveaxis((codes * scale).reshape(v.shape), -1, axis)


WIDE = False


def mx_kscale(k):
    if not WIDE:
        return np.ones(k)
    levels = np.array([10, -10, 5, -5, 0])
    if k % 512:
        return np.exp2(np.random.permutation(np.resize(levels, k // 32))).repeat(32)
    a = np.empty((k // 512, 16))
    for p in range(k // 512):
        a[p, :8] = np.random.permutation(np.resize(levels, 8))
        for g in range(8):
            far = levels[np.abs(levels - a[p, g]) >= 10]
            a[p, g + 8] = far[np.random.randint(len(far))]
    return np.exp2(a.ravel()).repeat(32)


def f64(x):
    return np.asarray(x).astype(np.float64)


def striped(idx):
    return np.tile(np.asarray(idx).reshape(-1, 16).T, (8, 1)).astype(np.uint16)


def unstriped(offs):
    return offs[:16].T.reshape(-1).astype(np.int64)


E2M1 = np.array([0.0, 0.5, 1.0, 1.5, 2.0, 3.0, 4.0, 6.0, -0.0, -0.5, -1.0, -1.5, -2.0, -3.0, -4.0, -6.0])


def pack_weight(w, fmt):
    k, n = w.shape
    w = f64(np.asarray(w, np.float32).astype(ml_dtypes.bfloat16)).reshape(k // 32, 32, n)
    amax = np.abs(w).max(1)
    if fmt == "e4m3":
        byte = np.frexp(amax)[1] - 1 + 127 - 7
    else:
        mant, ex = np.frexp(amax / 6.0)
        byte = np.where(mant > 0.5, ex, ex - 1) + 127
    byte = np.clip(np.where(amax > 0, byte, 1), 1, 254)
    scaled = (w * np.exp2(127.0 - byte)[:, None, :]).reshape(k, n).astype(np.float32)
    by_word = np.ascontiguousarray(scaled.reshape(k // 512, 128, 4, n).transpose(0, 1, 3, 2))
    if fmt == "e4m3":
        words = by_word.astype(ml_dtypes.float8_e4m3fn).view(np.uint8)
    else:
        c = by_word.astype(ml_dtypes.float4_e2m1fn).view(np.uint8) & 0xF
        words = (c[..., 0::2] | (c[..., 1::2] << 4)).reshape(k // 512, 128, 2 * n)
    return np.ascontiguousarray(words), np.ascontiguousarray(byte.astype(np.uint8).reshape(k // 512, 16, n))


def unpack_weight(words, scales, fmt):
    g, _, n = scales.shape
    words = np.ascontiguousarray(words).reshape(g, 128, n, -1)
    if fmt == "e4m3":
        vals = words.view(ml_dtypes.float8_e4m3fn).astype(np.float64)
    else:
        nib = np.empty((g, 128, n, 4), np.uint8)
        nib[..., 0::2] = words & 0xF
        nib[..., 1::2] = words >> 4
        vals = E2M1[nib]
    vals = vals * np.repeat(np.exp2(scales.astype(np.float64) - 127.0), 8, axis=1)[..., None]
    return vals.transpose(0, 1, 3, 2).reshape(g * 512, n)


def sigmoid(v):
    return 1.0 / (1.0 + np.exp(-v))


def bf(x):
    return np.asarray(x, np.float32).astype(ml_dtypes.bfloat16)


def planes(Y):
    r, m = Y.shape
    b = f64(bf(Y)).reshape(r // 32, 32, m)
    amax = np.abs(b).max(1)
    byte = np.clip(np.where(amax > 0, np.frexp(amax)[1] - 1 + 127 - 7, 1), 1, 254)
    codes = (b * np.exp2(127.0 - byte)[:, None, :]).reshape(r, m).astype(np.float32).astype(ml_dtypes.float8_e4m3fn).view(np.uint8)
    words = codes.reshape(r // 512, 128, 4, m).transpose(0, 1, 3, 2)
    return np.ascontiguousarray(words), np.ascontiguousarray(byte.astype(np.uint8).reshape(r // 512, 16, m))


K, R, F, T, J, G = 512, 512, 512, 2048, 256, 16


def setup_inputs():
    n = np.random.standard_normal
    idx = np.random.permutation(T)[:J]
    fk = mx_kscale(K)
    fr = mx_kscale(R)
    dtabp = pack_weight(n((K, T)) / fk[:, None], "e4m3")
    tabp = pack_weight(n((K, T)) / fk[:, None], "e4m3")
    return {
        "dtab_words": dtabp[0],
        "dtab_scales": dtabp[1],
        "tab_words": tabp[0],
        "tab_scales": tabp[1],
        "w1": (n((K, R)) * 1 / np.sqrt(K) * fk[:, None]).astype(np.float32),
        "steep": (np.random.uniform(1.0, 4.0, (R, 1))).astype(np.float32),
        "bias": (np.random.uniform(-0.5, 0.5, (R, 1))).astype(np.float32),
        "rs": (np.random.uniform(0.5, 2.0, (R, 1)) * fr[:, None]).astype(np.float32),
        "wor": (n((R, F)) * 1 / np.sqrt(R) / fr[:, None]).astype(np.float32),
        "res": (n((F, J)) * 0.5).astype(np.float32),
        "offs": striped(idx),
    }


def reference(dtab_words, dtab_scales, tab_words, tab_scales, w1, steep, bias, rs, wor, res, offs):
    idx = unstriped(offs)
    dtabu = unpack_weight(dtab_words, dtab_scales, "e4m3")
    tabu = unpack_weight(tab_words, tab_scales, "e4m3")
    w1q = mxq(f64(w1), 0, "e4m3")
    tabidxg = tabu[:, idx]
    a = w1q.T @ tabidxg
    dtabidxg = dtabu[:, idx]
    ta = w1q.T @ dtabidxg
    m1 = a.reshape(R, G, J // G).mean(axis=2)
    gt = sigmoid(m1 * f64(steep) + f64(bias))
    gr0 = np.repeat(gt, J // G, axis=1)
    tm1 = ta.reshape(R, G, J // G).mean(axis=2)
    tgt = tm1 * f64(steep) * gt * (1.0 - gt)
    tgr0 = np.repeat(tgt, J // G, axis=1)
    tu1 = ta * gr0 + tgr0 * a
    fo1 = tu1 * f64(rs)
    worq = mxq(f64(wor), 0, "e4m3")
    fo1q = mxq(fo1, 0, "e4m3")
    yo = worq.T @ fo1q
    y = yo + f64(res)
    words, scales = planes(y)
    return y, words, scales

@@ -1,0 +1,255 @@
+from contextlib import ExitStack
+
+import concourse.mybir as mybir
+
+K, R, F, T, J, G = 512, 512, 512, 2048, 256, 16
+
+F32 = mybir.dt.float32
+BF16 = mybir.dt.bfloat16
+I32 = mybir.dt.int32
+U32 = mybir.dt.uint32
+U16 = mybir.dt.uint16
+U8 = mybir.dt.uint8
+FP8X4 = mybir.dt.float8_e4m3fn_x4
+ALU = mybir.AluOpType
+ACT = mybir.ActivationFunctionType
+AXIS_X = mybir.AxisListType.X
+
+P = 128
+PACK = 4
+GROUP = J // G
+HALVES = 2
+JH = J // HALVES
+GH = G // HALVES
+QUADRANTS = 4
+
+FLOPS = 2 * K * R * J * 2 + 2 * R * F * J
+
+
+def tile_attend_tsqueeze_o_pl_kernel(
+    tc, dtab_words, dtab_scales, tab_words, tab_scales, w1, steep, bias, rs, wor, res, offs, out_0, out_1, out_2
+):
+    nc = tc.nc
+    with ExitStack() as ctx:
+        sb = ctx.enter_context(tc.tile_pool(name="sb", bufs=1))
+        ps = ctx.enter_context(tc.psum_pool(name="ps", bufs=1))
+
+        def mx_tile(shape, dtype, name, tag=None):
+            return sb.tile(shape, dtype, name=name, tag=tag or name, align_bytes=64)
+
+        def words_view(words):
+            return words[0].rearrange("p n t -> p (n t)").bitcast(I32)
+
+        def load_scale_rows(queue, plane, scales):
+            for q in range(QUADRANTS):
+                queue.dma_start(
+                    out=plane[32 * q : 32 * q + PACK, :].bitcast(I32),
+                    in_=scales[0, PACK * q : PACK * (q + 1), :].bitcast(I32),
+                )
+
+        def load_per_feature(vector, name):
+            tile = sb.tile([P, PACK], F32, name=name)
+            nc.scalar.dma_start(out=tile[:], in_=vector.rearrange("(p t) o -> p (t o)", t=PACK))
+            return tile
+
+        warm_in = sb.tile([P, 1], F32, name="warm_in")
+        warm_out = sb.tile([P, 1], F32, name="warm_out")
+        nc.vector.memset(warm_in[:], 0.0)
+        tab_plane = mx_tile([P, T], U8, "tab_plane")
+        dtab_plane = mx_tile([P, T], U8, "dtab_plane")
+        nc.vector.memset(dtab_plane[:].bitcast(I32), 0)
+        nc.vector.memset(tab_plane[:].bitcast(I32), 0)
+
+        w1_raw = sb.tile([P, PACK, R], F32, name="w1_raw", tag="weight_raw")
+        nc.sync.dma_start(out=w1_raw[:], in_=w1.rearrange("(p s) r -> p s r", s=PACK))
+        offsets = sb.tile([P, J // 16], U16, name="offsets")
+        nc.sync.dma_start(offsets[:], offs)
+        steep_sb = load_per_feature(steep, "steep_sb")
+        bias_sb = load_per_feature(bias, "bias_sb")
+        rs_sb = load_per_feature(rs, "rs_sb")
+        nc.scalar.activation(out=warm_out[:], in_=warm_in[:], func=ACT.Sigmoid)
+        load_scale_rows(nc.scalar, tab_plane, tab_scales)
+        load_scale_rows(nc.gpsimd, dtab_plane, dtab_scales)
+        tab_pool = mx_tile([P, T], U32, "tab_pool")
+        nc.sync.dma_start(out=tab_pool[:].bitcast(I32), in_=words_view(tab_words))
+        dtab_pool = mx_tile([P, T], U32, "dtab_pool")
+        nc.sync.dma_start(out=dtab_pool[:].bitcast(I32), in_=words_view(dtab_words))
+
+        mean_steep = sb.tile([P, PACK], F32, name="mean_steep")
+        slope = sb.tile([P, PACK], F32, name="slope")
+        neg_slope = sb.tile([P, PACK], F32, name="neg_slope")
+        nc.gpsimd.tensor_scalar(mean_steep[:], steep_sb[:], 1.0 / GROUP, 0.0, ALU.mult, ALU.add)
+        nc.gpsimd.tensor_tensor(slope[:], mean_steep[:], rs_sb[:], ALU.mult)
+        nc.gpsimd.tensor_scalar(neg_slope[:], slope[:], -1.0, 0.0, ALU.mult, ALU.add)
+
+        def deal(copy, raw, pair, name):
+            grouped = mx_tile([P, 2, P, PACK], BF16, name)
+            copy(
+                out=grouped[:].rearrange("p t m s -> p m s t"),
+                in_=raw[:].rearrange("p s (m t) -> p m s t", t=PACK)[:, :, :, 2 * pair : 2 * pair + 2],
+            )
+            return grouped
+
+        def quantize_pair(grouped, codes, plane, pair):
+            cols = slice(2 * P * pair, 2 * P * (pair + 1))
+            nc.vector.quantize_mx(
+                out=codes[:, cols].bitcast(FP8X4),
+                scales=plane[:, cols],
+                in_=grouped[:].rearrange("p t m s -> p (t m s)"),
+            )
+
+        def gather(pool, dtype, name):
+            picked = mx_tile([P, J], dtype, name)
+            nc.vector.tensor_copy(out=picked[:], in_=pool[:].indirect(offsets[:]))
+            return picked
+
+        def product(w_codes, w_plane, x_codes, x_plane, half, name):
+            bank = ps.tile([P, PACK, JH], F32, name=name)
+            cols = slice(JH * half, JH * (half + 1))
+            for t in range(PACK):
+                nc.tensor.matmul_mx(
+                    out=bank[:, t, :],
+                    lhsT=w_codes[:, P * t : P * (t + 1)].bitcast(FP8X4),
+                    lhsT_scale=w_plane[:, P * t : P * (t + 1)],
+                    rhs=x_codes[:, cols].bitcast(FP8X4),
+                    rhs_scale=x_plane[:, cols],
+                    start=True,
+                    stop=True,
+                )
+            return bank
+
+        w1_codes = mx_tile([P, R], U32, "w1_codes")
+        w1_plane = mx_tile([P, R], U8, "w1_plane")
+        w1_low = deal(nc.vector.tensor_copy, w1_raw, 0, "w1_low")
+        w1_high = deal(nc.scalar.copy, w1_raw, 1, "w1_high")
+        quantize_pair(w1_low, w1_codes, w1_plane, 0)
+        tab_picked_plane = gather(tab_plane, U8, "tab_picked_plane")
+        quantize_pair(w1_high, w1_codes, w1_plane, 1)
+        wor_raw = sb.tile([P, PACK, F], F32, name="wor_raw", tag="weight_raw")
+        nc.sync.dma_start(out=wor_raw[:], in_=wor.rearrange("(p s) f -> p s f", s=PACK))
+        res_sb = mx_tile([P, PACK, J], F32, "res_sb", tag="w1_high")
+        nc.sync.dma_start(out=res_sb[:], in_=res.rearrange("(p t) j -> p t j", t=PACK))
+        tab_picked = gather(tab_pool, U32, "tab_picked")
+        a_banks = [product(w1_codes, w1_plane, tab_picked, tab_picked_plane, h, "a_bank%d" % h) for h in range(HALVES)]
+        dtab_picked_plane = gather(dtab_plane, U8, "dtab_picked_plane")
+
+        a_sum = sb.tile([P, PACK, G], F32, name="a_sum")
+        for h in range(HALVES):
+            nc.vector.tensor_reduce(
+                out=a_sum[:, :, GH * h : GH * (h + 1)],
+                in_=a_banks[h][:].rearrange("p t (g i) -> p t g i", i=GROUP),
+                axis=AXIS_X,
+                op=ALU.add,
+            )
+        dtab_picked = gather(dtab_pool, U32, "dtab_picked")
+        ta_banks = [
+            product(w1_codes, w1_plane, dtab_picked, dtab_picked_plane, h, "ta_bank%d" % h) for h in range(HALVES)
+        ]
+
+        gate = sb.tile([P, PACK, G], F32, name="gate")
+        rest = sb.tile([P, PACK, G], F32, name="rest")
+        for t in range(PACK):
+            nc.scalar.activation(
+                out=gate[:, t, :],
+                in_=a_sum[:, t, :],
+                func=ACT.Sigmoid,
+                bias=bias_sb[:, t : t + 1],
+                scale=mean_steep[:, t : t + 1],
+            )
+        for t in range(PACK):
+            nc.scalar.activation(
+                out=rest[:, t, :],
+                in_=gate[:, t, :],
+                func=ACT.Identity,
+                bias=slope[:, t : t + 1],
+                scale=neg_slope[:, t : t + 1],
+            )
+        ta_factor = sb.tile([P, G, PACK], F32, name="ta_factor")
+        sum_factor = sb.tile([P, G, PACK], F32, name="sum_factor")
+        gate_gt = gate[:].rearrange("p t g -> p g t")
+        nc.vector.tensor_tensor(
+            ta_factor[:], gate_gt, rs_sb[:].unsqueeze(1).to_broadcast([P, G, PACK]), ALU.mult
+        )
+        nc.vector.tensor_tensor(sum_factor[:], gate_gt, rest[:].rearrange("p t g -> p g t"), ALU.mult)
+
+        wor_codes = mx_tile([P, F], U32, "wor_codes")
+        wor_plane = mx_tile([P, F], U8, "wor_plane")
+        wor_low = deal(nc.scalar.copy, wor_raw, 0, "wor_low")
+        wor_high = deal(nc.scalar.copy, wor_raw, 1, "wor_high")
+
+        def times_group_factor(bank, factor, name):
+            scaled = sb.tile([P, GH, GROUP, PACK], F32, name=name)
+            nc.vector.tensor_tensor(
+                scaled[:],
+                bank[:].rearrange("p t (g i) -> p g i t", i=GROUP),
+                factor.unsqueeze(2).to_broadcast([P, GH, GROUP, PACK]),
+                ALU.mult,
+            )
+            return scaled
+
+        ta_sums, a_factors, ta_terms, a_terms, fo_grouped = [], [], [], [], []
+        for h in range(HALVES):
+            ta_sum = sb.tile([P, GH, PACK], F32, name="ta_sum%d" % h)
+            nc.vector.tensor_reduce(
+                out=ta_sum[:],
+                in_=ta_banks[h][:].rearrange("p t (g i) -> p g t i", i=GROUP),
+                axis=AXIS_X,
+                op=ALU.add,
+            )
+            ta_sums.append(ta_sum)
+        for h in range(HALVES):
+            groups = slice(GH * h, GH * (h + 1))
+            a_factor = sb.tile([P, GH, PACK], F32, name="a_factor%d" % h)
+            nc.vector.tensor_tensor(a_factor[:], ta_sums[h][:], sum_factor[:, groups, :], ALU.mult)
+            a_factors.append(a_factor)
+            ta_terms.append(times_group_factor(ta_banks[h], ta_factor[:, groups, :], "ta_term%d" % h))
+        for h in range(HALVES):
+            a_terms.append(times_group_factor(a_banks[h], a_factors[h][:], "a_term%d" % h))
+        fo_codes = mx_tile([P, J], U32, "fo_codes")
+        fo_plane = mx_tile([P, J], U8, "fo_plane")
+        for h in range(HALVES):
+            grouped = mx_tile([P, JH * PACK], BF16, "fo_grouped%d" % h)
+            nc.vector.tensor_tensor(
+                grouped[:],
+                ta_terms[h][:].rearrange("p g i t -> p (g i t)"),
+                a_terms[h][:].rearrange("p g i t -> p (g i t)"),
+                ALU.add,
+            )
+            fo_grouped.append(grouped)
+            quantize_pair((wor_low, wor_high)[h], wor_codes, wor_plane, h)
+        yo_banks = []
+        for h in range(HALVES):
+            cols = slice(JH * h, JH * (h + 1))
+            nc.vector.quantize_mx(out=fo_codes[:, cols].bitcast(FP8X4), scales=fo_plane[:, cols], in_=fo_grouped[h][:])
+            yo_banks.append(product(wor_codes, wor_plane, fo_codes, fo_plane, h, "yo_bank%d" % h))
+
+        y_codes = mx_tile([P, J], U32, "y_codes")
+        y_plane = mx_tile([P, J], U8, "y_plane")
+        out_rows = out_0.rearrange("(p t) j -> p t j", t=PACK)
+        y_grouped = []
+        for h in range(HALVES):
+            cols = slice(JH * h, JH * (h + 1))
+            y = sb.tile([P, PACK, JH], F32, name="y%d" % h)
+            nc.vector.tensor_tensor(y[:], yo_banks[h][:], res_sb[:, :, cols], ALU.add)
+            nc.sync.dma_start(out=out_rows[:, :, cols], in_=y[:])
+            grouped = mx_tile([P, JH, PACK], BF16, "y_grouped%d" % h)
+            copy = (nc.scalar.copy, nc.vector.tensor_copy)[h]
+            copy(
+                out=grouped[:].rearrange("p (c i) t -> p c t i", i=4),
+                in_=y[:].rearrange("p t (c i) -> p c t i", i=4),
+            )
+            y_grouped.append(grouped)
+        for h in range(HALVES):
+            cols = slice(JH * h, JH * (h + 1))
+            nc.vector.quantize_mx(
+                out=y_codes[:, cols].bitcast(FP8X4),
+                scales=y_plane[:, cols],
+                in_=y_grouped[h][:].rearrange("p j t -> p (j t)"),
+            )
+        nc.sync.dma_start(out=words_view(out_1), in_=y_codes[:].bitcast(I32))
+        for q in range(QUADRANTS):
+            queue = (nc.scalar, nc.sync)[q % 2]
+            queue.dma_start(
+                out=out_2[0, PACK * q : PACK * (q + 1), :].bitcast(I32),
+                in_=y_plane[32 * q : 32 * q + PACK, :].bitcast(I32),
+            )

@@ -22,6 +22,7 @@ HALVES = 2
 JH = J // HALVES
 GH = G // HALVES
 QUADRANTS = 4
+DTAB_ROW = 4
 
 FLOPS = 2 * K * R * J * 2 + 2 * R * F * J
 
@@ -40,25 +41,25 @@ def tile_attend_tsqueeze_o_pl_kernel(
         def words_view(words):
             return words[0].rearrange("p n t -> p (n t)").bitcast(I32)
 
-        def load_scale_rows(queue, plane, scales):
+        def load_scale_rows(queue, plane, scales, first_row):
             for q in range(QUADRANTS):
                 queue.dma_start(
-                    out=plane[32 * q : 32 * q + PACK, :].bitcast(I32),
+                    out=plane[32 * q + first_row : 32 * q + first_row + PACK, :].bitcast(I32),
                     in_=scales[0, PACK * q : PACK * (q + 1), :].bitcast(I32),
                 )
 
         def load_per_feature(vector, name):
             tile = sb.tile([P, PACK], F32, name=name)
-            nc.scalar.dma_start(out=tile[:], in_=vector.rearrange("(p t) o -> p (t o)", t=PACK))
+            nc.gpsimd.dma_start(out=tile[:], in_=vector.rearrange("(p t) o -> p (t o)", t=PACK))
             return tile
 
-        warm_in = sb.tile([P, 1], F32, name="warm_in")
-        warm_out = sb.tile([P, 1], F32, name="warm_out")
+        warm_in = mx_tile([P, 1], F32, "warm_in", tag="tab_pool")
+        warm_out = mx_tile([P, 1], F32, "warm_out", tag="dtab_pool")
         nc.vector.memset(warm_in[:], 0.0)
         tab_plane = mx_tile([P, T], U8, "tab_plane")
         dtab_plane = mx_tile([P, T], U8, "dtab_plane")
-        nc.vector.memset(dtab_plane[:].bitcast(I32), 0)
         nc.vector.memset(tab_plane[:].bitcast(I32), 0)
+        nc.vector.memset(dtab_plane[:].bitcast(I32), 0)
 
         w1_raw = sb.tile([P, PACK, R], F32, name="w1_raw", tag="weight_raw")
         nc.sync.dma_start(out=w1_raw[:], in_=w1.rearrange("(p s) r -> p s r", s=PACK))
@@ -68,8 +69,8 @@ def tile_attend_tsqueeze_o_pl_kernel(
         bias_sb = load_per_feature(bias, "bias_sb")
         rs_sb = load_per_feature(rs, "rs_sb")
         nc.scalar.activation(out=warm_out[:], in_=warm_in[:], func=ACT.Sigmoid)
-        load_scale_rows(nc.scalar, tab_plane, tab_scales)
-        load_scale_rows(nc.gpsimd, dtab_plane, dtab_scales)
+        load_scale_rows(nc.sync, tab_plane, tab_scales, 0)
+        load_scale_rows(nc.scalar, dtab_plane, dtab_scales, DTAB_ROW)
         tab_pool = mx_tile([P, T], U32, "tab_pool")
         nc.sync.dma_start(out=tab_pool[:].bitcast(I32), in_=words_view(tab_words))
         dtab_pool = mx_tile([P, T], U32, "dtab_pool")
@@ -98,8 +99,8 @@ def tile_attend_tsqueeze_o_pl_kernel(
                 in_=grouped[:].rearrange("p t m s -> p (t m s)"),
             )
 
-        def gather(pool, dtype, name):
-            picked = mx_tile([P, J], dtype, name)
+        def gather(pool, dtype, name, tag=None):
+            picked = mx_tile([P, J], dtype, name, tag)
             nc.vector.tensor_copy(out=picked[:], in_=pool[:].indirect(offsets[:]))
             return picked
 
@@ -131,7 +132,7 @@ def tile_attend_tsqueeze_o_pl_kernel(
         nc.sync.dma_start(out=res_sb[:], in_=res.rearrange("(p t) j -> p t j", t=PACK))
         tab_picked = gather(tab_pool, U32, "tab_picked")
         a_banks = [product(w1_codes, w1_plane, tab_picked, tab_picked_plane, h, "a_bank%d" % h) for h in range(HALVES)]
-        dtab_picked_plane = gather(dtab_plane, U8, "dtab_picked_plane")
+        dtab_picked_plane = gather(dtab_plane, U8, "dtab_picked_plane", tag="tab_pool")
 
         a_sum = sb.tile([P, PACK, G], F32, name="a_sum")
         for h in range(HALVES):
@@ -143,7 +144,7 @@ def tile_attend_tsqueeze_o_pl_kernel(
             )
         dtab_picked = gather(dtab_pool, U32, "dtab_picked")
         ta_banks = [
-            product(w1_codes, w1_plane, dtab_picked, dtab_picked_plane, h, "ta_bank%d" % h) for h in range(HALVES)
+            product(w1_codes, w1_plane, dtab_picked, dtab_picked_plane[DTAB_ROW:P, :], h, "ta_bank%d" % h) for h in range(HALVES)
         ]
 
         gate = sb.tile([P, PACK, G], F32, name="gate")
@@ -187,7 +188,7 @@ def tile_attend_tsqueeze_o_pl_kernel(
             )
             return scaled
 
-        ta_sums, a_factors, ta_terms, a_terms, fo_grouped = [], [], [], [], []
+        ta_sums, a_factors, ta_terms, a_terms = [], [], [], []
         for h in range(HALVES):
             ta_sum = sb.tile([P, GH, PACK], F32, name="ta_sum%d" % h)
             nc.vector.tensor_reduce(
@@ -215,13 +216,10 @@ def tile_attend_tsqueeze_o_pl_kernel(
                 a_terms[h][:].rearrange("p g i t -> p (g i t)"),
                 ALU.add,
             )
-            fo_grouped.append(grouped)
             quantize_pair((wor_low, wor_high)[h], wor_codes, wor_plane, h)
-        yo_banks = []
-        for h in range(HALVES):
             cols = slice(JH * h, JH * (h + 1))
-            nc.vector.quantize_mx(out=fo_codes[:, cols].bitcast(FP8X4), scales=fo_plane[:, cols], in_=fo_grouped[h][:])
-            yo_banks.append(product(wor_codes, wor_plane, fo_codes, fo_plane, h, "yo_bank%d" % h))
+            nc.vector.quantize_mx(out=fo_codes[:, cols].bitcast(FP8X4), scales=fo_plane[:, cols], in_=grouped[:])
+        yo_banks = [product(wor_codes, wor_plane, fo_codes, fo_plane, h, "yo_bank%d" % h) for h in range(HALVES)]
 
         y_codes = mx_tile([P, J], U32, "y_codes")
         y_plane = mx_tile([P, J], U8, "y_plane")

@@ -49,19 +49,17 @@ def tile_attend_tsqueeze_o_pl_kernel(
                 )
 
         def load_per_feature(vector, name):
-            tile = sb.tile([P, PACK], F32, name=name)
+            tile = mx_tile([P, PACK], F32, name)
             nc.gpsimd.dma_start(out=tile[:], in_=vector.rearrange("(p t) o -> p (t o)", t=PACK))
             return tile
 
         warm_in = mx_tile([P, 1], F32, "warm_in", tag="tab_pool")
-        warm_out = mx_tile([P, 1], F32, "warm_out", tag="dtab_pool")
-        nc.vector.memset(warm_in[:], 0.0)
+        warm_out = mx_tile([P, 1], F32, "warm_out", tag="dtab_plane")
         tab_plane = mx_tile([P, T], U8, "tab_plane")
-        dtab_plane = mx_tile([P, T], U8, "dtab_plane")
         nc.vector.memset(tab_plane[:].bitcast(I32), 0)
-        nc.vector.memset(dtab_plane[:].bitcast(I32), 0)
+        nc.vector.memset(warm_in[:], 0.0)
 
-        w1_raw = sb.tile([P, PACK, R], F32, name="w1_raw", tag="weight_raw")
+        w1_raw = mx_tile([P, PACK, R], F32, "w1_raw")
         nc.sync.dma_start(out=w1_raw[:], in_=w1.rearrange("(p s) r -> p s r", s=PACK))
         offsets = sb.tile([P, J // 16], U16, name="offsets")
         nc.sync.dma_start(offsets[:], offs)
@@ -70,16 +68,18 @@ def tile_attend_tsqueeze_o_pl_kernel(
         rs_sb = load_per_feature(rs, "rs_sb")
         nc.scalar.activation(out=warm_out[:], in_=warm_in[:], func=ACT.Sigmoid)
         load_scale_rows(nc.sync, tab_plane, tab_scales, 0)
-        load_scale_rows(nc.scalar, dtab_plane, dtab_scales, DTAB_ROW)
         tab_pool = mx_tile([P, T], U32, "tab_pool")
         nc.sync.dma_start(out=tab_pool[:].bitcast(I32), in_=words_view(tab_words))
-        dtab_pool = mx_tile([P, T], U32, "dtab_pool")
-        nc.sync.dma_start(out=dtab_pool[:].bitcast(I32), in_=words_view(dtab_words))
+        dtab_plane = mx_tile([P, T], U8, "dtab_plane")
+        nc.vector.memset(dtab_plane[:].bitcast(I32), 0)
+        load_scale_rows(nc.sync, dtab_plane, dtab_scales, DTAB_ROW)
 
         mean_steep = sb.tile([P, PACK], F32, name="mean_steep")
         slope = sb.tile([P, PACK], F32, name="slope")
         neg_slope = sb.tile([P, PACK], F32, name="neg_slope")
         nc.gpsimd.tensor_scalar(mean_steep[:], steep_sb[:], 1.0 / GROUP, 0.0, ALU.mult, ALU.add)
+        dtab_pool = mx_tile([P, T], U32, "dtab_pool", tag="steep_sb")
+        nc.sync.dma_start(out=dtab_pool[:].bitcast(I32), in_=words_view(dtab_words))
         nc.gpsimd.tensor_tensor(slope[:], mean_steep[:], rs_sb[:], ALU.mult)
         nc.gpsimd.tensor_scalar(neg_slope[:], slope[:], -1.0, 0.0, ALU.mult, ALU.add)
 
@@ -126,52 +126,62 @@ def tile_attend_tsqueeze_o_pl_kernel(
         quantize_pair(w1_low, w1_codes, w1_plane, 0)
         tab_picked_plane = gather(tab_plane, U8, "tab_picked_plane")
         quantize_pair(w1_high, w1_codes, w1_plane, 1)
-        wor_raw = sb.tile([P, PACK, F], F32, name="wor_raw", tag="weight_raw")
+        wor_raw = mx_tile([P, PACK, F], F32, "wor_raw", tag="w1_raw")
         nc.sync.dma_start(out=wor_raw[:], in_=wor.rearrange("(p s) f -> p s f", s=PACK))
-        res_sb = mx_tile([P, PACK, J], F32, "res_sb", tag="w1_high")
-        nc.sync.dma_start(out=res_sb[:], in_=res.rearrange("(p t) j -> p t j", t=PACK))
         tab_picked = gather(tab_pool, U32, "tab_picked")
+        res_sb = mx_tile([P, PACK, J], F32, "res_sb", tag="tab_pool")
+        nc.sync.dma_start(out=res_sb[:], in_=res.rearrange("(p t) j -> p t j", t=PACK))
         a_banks = [product(w1_codes, w1_plane, tab_picked, tab_picked_plane, h, "a_bank%d" % h) for h in range(HALVES)]
-        dtab_picked_plane = gather(dtab_plane, U8, "dtab_picked_plane", tag="tab_pool")
+        dtab_picked_plane = gather(dtab_plane, U8, "dtab_picked_plane")
 
-        a_sum = sb.tile([P, PACK, G], F32, name="a_sum")
-        for h in range(HALVES):
+        def group_sums(bank, order, name, tag=None):
+            shape = [P, PACK, GH] if order == "t g" else [P, GH, PACK]
+            sums = mx_tile(shape, F32, name, tag)
             nc.vector.tensor_reduce(
-                out=a_sum[:, :, GH * h : GH * (h + 1)],
-                in_=a_banks[h][:].rearrange("p t (g i) -> p t g i", i=GROUP),
+                out=sums[:],
+                in_=bank[:].rearrange("p t (g i) -> p %s i" % order, i=GROUP),
                 axis=AXIS_X,
                 op=ALU.add,
             )
+            return sums
+
+        a_sums = [group_sums(a_banks[0], "t g", "a_sum0")]
         dtab_picked = gather(dtab_pool, U32, "dtab_picked")
+        a_sums.append(group_sums(a_banks[1], "t g", "a_sum1", tag="steep_sb"))
         ta_banks = [
-            product(w1_codes, w1_plane, dtab_picked, dtab_picked_plane[DTAB_ROW:P, :], h, "ta_bank%d" % h) for h in range(HALVES)
+            product(w1_codes, w1_plane, dtab_picked, dtab_picked_plane[DTAB_ROW:P, :], h, "ta_bank%d" % h)
+            for h in range(HALVES)
         ]
 
-        gate = sb.tile([P, PACK, G], F32, name="gate")
-        rest = sb.tile([P, PACK, G], F32, name="rest")
-        for t in range(PACK):
-            nc.scalar.activation(
-                out=gate[:, t, :],
-                in_=a_sum[:, t, :],
-                func=ACT.Sigmoid,
-                bias=bias_sb[:, t : t + 1],
-                scale=mean_steep[:, t : t + 1],
+        ta_factors, sum_factors = [], []
+        for h in range(HALVES):
+            gate = sb.tile([P, PACK, GH], F32, name="gate%d" % h)
+            rest = sb.tile([P, PACK, GH], F32, name="rest%d" % h)
+            for t in range(PACK):
+                nc.scalar.activation(
+                    out=gate[:, t, :],
+                    in_=a_sums[h][:, t, :],
+                    func=ACT.Sigmoid,
+                    bias=bias_sb[:, t : t + 1],
+                    scale=mean_steep[:, t : t + 1],
+                )
+            for t in range(PACK):
+                nc.scalar.activation(
+                    out=rest[:, t, :],
+                    in_=gate[:, t, :],
+                    func=ACT.Identity,
+                    bias=slope[:, t : t + 1],
+                    scale=neg_slope[:, t : t + 1],
+                )
+            ta_factor = sb.tile([P, GH, PACK], F32, name="ta_factor%d" % h)
+            sum_factor = sb.tile([P, GH, PACK], F32, name="sum_factor%d" % h)
+            gate_by_group = gate[:].rearrange("p t g -> p g t")
+            nc.gpsimd.tensor_tensor(
+                ta_factor[:], gate_by_group, rs_sb[:].unsqueeze(1).to_broadcast([P, GH, PACK]), ALU.mult
             )
-        for t in range(PACK):
-            nc.scalar.activation(
-                out=rest[:, t, :],
-                in_=gate[:, t, :],
-                func=ACT.Identity,
-                bias=slope[:, t : t + 1],
-                scale=neg_slope[:, t : t + 1],
-            )
-        ta_factor = sb.tile([P, G, PACK], F32, name="ta_factor")
-        sum_factor = sb.tile([P, G, PACK], F32, name="sum_factor")
-        gate_gt = gate[:].rearrange("p t g -> p g t")
-        nc.vector.tensor_tensor(
-            ta_factor[:], gate_gt, rs_sb[:].unsqueeze(1).to_broadcast([P, G, PACK]), ALU.mult
-        )
-        nc.vector.tensor_tensor(sum_factor[:], gate_gt, rest[:].rearrange("p t g -> p g t"), ALU.mult)
+            nc.gpsimd.tensor_tensor(sum_factor[:], gate_by_group, rest[:].rearrange("p t g -> p g t"), ALU.mult)
+            ta_factors.append(ta_factor)
+            sum_factors.append(sum_factor)
 
         wor_codes = mx_tile([P, F], U32, "wor_codes")
         wor_plane = mx_tile([P, F], U8, "wor_plane")
@@ -188,37 +198,39 @@ def tile_attend_tsqueeze_o_pl_kernel(
             )
             return scaled
 
-        ta_sums, a_factors, ta_terms, a_terms = [], [], [], []
+        a_factors = []
         for h in range(HALVES):
-            ta_sum = sb.tile([P, GH, PACK], F32, name="ta_sum%d" % h)
-            nc.vector.tensor_reduce(
-                out=ta_sum[:],
-                in_=ta_banks[h][:].rearrange("p t (g i) -> p g t i", i=GROUP),
-                axis=AXIS_X,
-                op=ALU.add,
-            )
-            ta_sums.append(ta_sum)
-        for h in range(HALVES):
-            groups = slice(GH * h, GH * (h + 1))
+            ta_sum = group_sums(ta_banks[h], "g t", "ta_sum%d" % h)
             a_factor = sb.tile([P, GH, PACK], F32, name="a_factor%d" % h)
-            nc.vector.tensor_tensor(a_factor[:], ta_sums[h][:], sum_factor[:, groups, :], ALU.mult)
+            nc.gpsimd.tensor_tensor(a_factor[:], ta_sum[:], sum_factors[h][:], ALU.mult)
             a_factors.append(a_factor)
-            ta_terms.append(times_group_factor(ta_banks[h], ta_factor[:, groups, :], "ta_term%d" % h))
-        for h in range(HALVES):
-            a_terms.append(times_group_factor(a_banks[h], a_factors[h][:], "a_term%d" % h))
         fo_codes = mx_tile([P, J], U32, "fo_codes")
         fo_plane = mx_tile([P, J], U8, "fo_plane")
-        for h in range(HALVES):
-            grouped = mx_tile([P, JH * PACK], BF16, "fo_grouped%d" % h)
-            nc.vector.tensor_tensor(
+
+        def add_terms(engine, ta_term, a_term, name):
+            grouped = mx_tile([P, JH * PACK], BF16, name)
+            engine.tensor_tensor(
                 grouped[:],
-                ta_terms[h][:].rearrange("p g i t -> p (g i t)"),
-                a_terms[h][:].rearrange("p g i t -> p (g i t)"),
+                ta_term[:].rearrange("p g i t -> p (g i t)"),
+                a_term[:].rearrange("p g i t -> p (g i t)"),
                 ALU.add,
             )
-            quantize_pair((wor_low, wor_high)[h], wor_codes, wor_plane, h)
-            cols = slice(JH * h, JH * (h + 1))
-            nc.vector.quantize_mx(out=fo_codes[:, cols].bitcast(FP8X4), scales=fo_plane[:, cols], in_=grouped[:])
+            return grouped
+
+        def quantize_half(grouped, codes, plane, half):
+            cols = slice(JH * half, JH * (half + 1))
+            nc.vector.quantize_mx(out=codes[:, cols].bitcast(FP8X4), scales=plane[:, cols], in_=grouped)
+
+        ta_term0 = times_group_factor(ta_banks[0], ta_factors[0][:], "ta_term0")
+        quantize_pair(wor_low, wor_codes, wor_plane, 0)
+        a_term0 = times_group_factor(a_banks[0], a_factors[0][:], "a_term0")
+        fo_grouped0 = add_terms(nc.gpsimd, ta_term0, a_term0, "fo_grouped0")
+        ta_term1 = times_group_factor(ta_banks[1], ta_factors[1][:], "ta_term1")
+        a_term1 = times_group_factor(a_banks[1], a_factors[1][:], "a_term1")
+        quantize_pair(wor_high, wor_codes, wor_plane, 1)
+        quantize_half(fo_grouped0[:], fo_codes, fo_plane, 0)
+        fo_grouped1 = add_terms(nc.vector, ta_term1, a_term1, "fo_grouped1")
+        quantize_half(fo_grouped1[:], fo_codes, fo_plane, 1)
         yo_banks = [product(wor_codes, wor_plane, fo_codes, fo_plane, h, "yo_bank%d" % h) for h in range(HALVES)]
 
         y_codes = mx_tile([P, J], U32, "y_codes")

@@ -42,10 +42,10 @@ def tile_attend_tsqueeze_o_pl_kernel(
             return words[0].rearrange("p n t -> p (n t)").bitcast(I32)
 
         def load_scale_rows(queue, plane, scales, first_row):
-            for q in range(QUADRANTS):
+            for x in range(PACK):
                 queue.dma_start(
-                    out=plane[32 * q + first_row : 32 * q + first_row + PACK, :].bitcast(I32),
-                    in_=scales[0, PACK * q : PACK * (q + 1), :].bitcast(I32),
+                    out=plane[first_row + x : P : 32, :].bitcast(I32),
+                    in_=scales[0, x : PACK * QUADRANTS : PACK, :].bitcast(I32),
                 )
 
         def load_per_feature(vector, name):
@@ -222,14 +222,14 @@ def tile_attend_tsqueeze_o_pl_kernel(
             nc.vector.quantize_mx(out=codes[:, cols].bitcast(FP8X4), scales=plane[:, cols], in_=grouped)
 
         ta_term0 = times_group_factor(ta_banks[0], ta_factors[0][:], "ta_term0")
-        quantize_pair(wor_low, wor_codes, wor_plane, 0)
         a_term0 = times_group_factor(a_banks[0], a_factors[0][:], "a_term0")
         fo_grouped0 = add_terms(nc.gpsimd, ta_term0, a_term0, "fo_grouped0")
         ta_term1 = times_group_factor(ta_banks[1], ta_factors[1][:], "ta_term1")
         a_term1 = times_group_factor(a_banks[1], a_factors[1][:], "a_term1")
-        quantize_pair(wor_high, wor_codes, wor_plane, 1)
+        quantize_pair(wor_low, wor_codes, wor_plane, 0)
         quantize_half(fo_grouped0[:], fo_codes, fo_plane, 0)
         fo_grouped1 = add_terms(nc.vector, ta_term1, a_term1, "fo_grouped1")
+        quantize_pair(wor_high, wor_codes, wor_plane, 1)
         quantize_half(fo_grouped1[:], fo_codes, fo_plane, 1)
         yo_banks = [product(wor_codes, wor_plane, fo_codes, fo_plane, h, "yo_bank%d" % h) for h in range(HALVES)]
 

@@ -48,9 +48,9 @@ def tile_attend_tsqueeze_o_pl_kernel(
                     in_=scales[0, x : PACK * QUADRANTS : PACK, :].bitcast(I32),
                 )
 
-        def load_per_feature(vector, name):
+        def load_per_feature(queue, vector, name):
             tile = mx_tile([P, PACK], F32, name)
-            nc.gpsimd.dma_start(out=tile[:], in_=vector.rearrange("(p t) o -> p (t o)", t=PACK))
+            queue.dma_start(out=tile[:], in_=vector.rearrange("(p t) o -> p (t o)", t=PACK))
             return tile
 
         warm_in = mx_tile([P, 1], F32, "warm_in", tag="tab_pool")
@@ -63,9 +63,9 @@ def tile_attend_tsqueeze_o_pl_kernel(
         nc.sync.dma_start(out=w1_raw[:], in_=w1.rearrange("(p s) r -> p s r", s=PACK))
         offsets = sb.tile([P, J // 16], U16, name="offsets")
         nc.sync.dma_start(offsets[:], offs)
-        steep_sb = load_per_feature(steep, "steep_sb")
-        bias_sb = load_per_feature(bias, "bias_sb")
-        rs_sb = load_per_feature(rs, "rs_sb")
+        steep_sb = load_per_feature(nc.sync, steep, "steep_sb")
+        rs_sb = load_per_feature(nc.gpsimd, rs, "rs_sb")
+        bias_sb = load_per_feature(nc.gpsimd, bias, "bias_sb")
         nc.scalar.activation(out=warm_out[:], in_=warm_in[:], func=ACT.Sigmoid)
         load_scale_rows(nc.sync, tab_plane, tab_scales, 0)
         tab_pool = mx_tile([P, T], U32, "tab_pool")
@@ -77,7 +77,7 @@ def tile_attend_tsqueeze_o_pl_kernel(
         mean_steep = sb.tile([P, PACK], F32, name="mean_steep")
         slope = sb.tile([P, PACK], F32, name="slope")
         neg_slope = sb.tile([P, PACK], F32, name="neg_slope")
-        nc.gpsimd.tensor_scalar(mean_steep[:], steep_sb[:], 1.0 / GROUP, 0.0, ALU.mult, ALU.add)
+        nc.scalar.mul(mean_steep[:], steep_sb[:], 1.0 / GROUP)
         dtab_pool = mx_tile([P, T], U32, "dtab_pool", tag="steep_sb")
         nc.sync.dma_start(out=dtab_pool[:].bitcast(I32), in_=words_view(dtab_words))
         nc.gpsimd.tensor_tensor(slope[:], mean_steep[:], rs_sb[:], ALU.mult)
@@ -175,11 +175,13 @@ def tile_attend_tsqueeze_o_pl_kernel(
                 )
             ta_factor = sb.tile([P, GH, PACK], F32, name="ta_factor%d" % h)
             sum_factor = sb.tile([P, GH, PACK], F32, name="sum_factor%d" % h)
-            gate_by_group = gate[:].rearrange("p t g -> p g t")
             nc.gpsimd.tensor_tensor(
-                ta_factor[:], gate_by_group, rs_sb[:].unsqueeze(1).to_broadcast([P, GH, PACK]), ALU.mult
+                sum_factor[:], gate[:].rearrange("p t g -> p g t"), rest[:].rearrange("p t g -> p g t"), ALU.mult
             )
-            nc.gpsimd.tensor_tensor(sum_factor[:], gate_by_group, rest[:].rearrange("p t g -> p g t"), ALU.mult)
+            for t in range(PACK):
+                nc.scalar.activation(
+                    out=ta_factor[:, :, t], in_=gate[:, t, :], func=ACT.Copy, scale=rs_sb[:, t : t + 1]
+                )
             ta_factors.append(ta_factor)
             sum_factors.append(sum_factor)
 

from contextlib import ExitStack

import concourse.mybir as mybir

K, R, F, T, J, G = 512, 512, 512, 2048, 256, 16

F32 = mybir.dt.float32
BF16 = mybir.dt.bfloat16
I32 = mybir.dt.int32
U32 = mybir.dt.uint32
U16 = mybir.dt.uint16
U8 = mybir.dt.uint8
FP8X4 = mybir.dt.float8_e4m3fn_x4
ALU = mybir.AluOpType
ACT = mybir.ActivationFunctionType
AXIS_X = mybir.AxisListType.X

P = 128
PACK = 4
GROUP = J // G
HALVES = 2
JH = J // HALVES
GH = G // HALVES
QUADRANTS = 4
DTAB_ROW = 4

FLOPS = 2 * K * R * J * 2 + 2 * R * F * J


def tile_attend_tsqueeze_o_pl_kernel(
    tc, dtab_words, dtab_scales, tab_words, tab_scales, w1, steep, bias, rs, wor, res, offs, out_0, out_1, out_2
):
    nc = tc.nc
    with ExitStack() as ctx:
        sb = ctx.enter_context(tc.tile_pool(name="sb", bufs=1))
        ps = ctx.enter_context(tc.psum_pool(name="ps", bufs=1))

        def mx_tile(shape, dtype, name, tag=None):
            return sb.tile(shape, dtype, name=name, tag=tag or name, align_bytes=64)

        def words_view(words):
            return words[0].rearrange("p n t -> p (n t)").bitcast(I32)

        def load_scale_rows(queue, plane, scales, first_row):
            for x in range(PACK):
                queue.dma_start(
                    out=plane[first_row + x : P : 32, :].bitcast(I32),
                    in_=scales[0, x : PACK * QUADRANTS : PACK, :].bitcast(I32),
                )

        def load_per_feature(queue, vector, name):
            tile = mx_tile([P, PACK], F32, name)
            queue.dma_start(out=tile[:], in_=vector.rearrange("(p t) o -> p (t o)", t=PACK))
            return tile

        warm_in = mx_tile([P, 1], F32, "warm_in", tag="tab_pool")
        warm_out = mx_tile([P, 1], F32, "warm_out", tag="dtab_plane")
        tab_plane = mx_tile([P, T], U8, "tab_plane")
        nc.vector.memset(tab_plane[:].bitcast(I32), 0)
        nc.vector.memset(warm_in[:], 0.0)

        w1_raw = mx_tile([P, PACK, R], F32, "w1_raw")
        nc.sync.dma_start(out=w1_raw[:], in_=w1.rearrange("(p s) r -> p s r", s=PACK))
        offsets = sb.tile([P, J // 16], U16, name="offsets")
        nc.sync.dma_start(offsets[:], offs)
        steep_sb = load_per_feature(nc.sync, steep, "steep_sb")
        rs_sb = load_per_feature(nc.gpsimd, rs, "rs_sb")
        bias_sb = load_per_feature(nc.gpsimd, bias, "bias_sb")
        nc.scalar.activation(out=warm_out[:], in_=warm_in[:], func=ACT.Sigmoid)
        load_scale_rows(nc.sync, tab_plane, tab_scales, 0)
        tab_pool = mx_tile([P, T], U32, "tab_pool")
        nc.sync.dma_start(out=tab_pool[:].bitcast(I32), in_=words_view(tab_words))
        dtab_plane = mx_tile([P, T], U8, "dtab_plane")
        nc.vector.memset(dtab_plane[:].bitcast(I32), 0)
        load_scale_rows(nc.sync, dtab_plane, dtab_scales, DTAB_ROW)

        mean_steep = sb.tile([P, PACK], F32, name="mean_steep")
        slope = sb.tile([P, PACK], F32, name="slope")
        neg_slope = sb.tile([P, PACK], F32, name="neg_slope")
        nc.scalar.mul(mean_steep[:], steep_sb[:], 1.0 / GROUP)
        dtab_pool = mx_tile([P, T], U32, "dtab_pool", tag="steep_sb")
        nc.sync.dma_start(out=dtab_pool[:].bitcast(I32), in_=words_view(dtab_words))
        nc.gpsimd.tensor_tensor(slope[:], mean_steep[:], rs_sb[:], ALU.mult)
        nc.gpsimd.tensor_scalar(neg_slope[:], slope[:], -1.0, 0.0, ALU.mult, ALU.add)

        def deal(copy, raw, pair, name):
            grouped = mx_tile([P, 2, P, PACK], BF16, name)
            copy(
                out=grouped[:].rearrange("p t m s -> p m s t"),
                in_=raw[:].rearrange("p s (m t) -> p m s t", t=PACK)[:, :, :, 2 * pair : 2 * pair + 2],
            )
            return grouped

        def quantize_pair(grouped, codes, plane, pair):
            cols = slice(2 * P * pair, 2 * P * (pair + 1))
            nc.vector.quantize_mx(
                out=codes[:, cols].bitcast(FP8X4),
                scales=plane[:, cols],
                in_=grouped[:].rearrange("p t m s -> p (t m s)"),
            )

        def gather(pool, dtype, name, tag=None):
            picked = mx_tile([P, J], dtype, name, tag)
            nc.vector.tensor_copy(out=picked[:], in_=pool[:].indirect(offsets[:]))
            return picked

        def product(w_codes, w_plane, x_codes, x_plane, half, name):
            bank = ps.tile([P, PACK, JH], F32, name=name)
            cols = slice(JH * half, JH * (half + 1))
            for t in range(PACK):
                nc.tensor.matmul_mx(
                    out=bank[:, t, :],
                    lhsT=w_codes[:, P * t : P * (t + 1)].bitcast(FP8X4),
                    lhsT_scale=w_plane[:, P * t : P * (t + 1)],
                    rhs=x_codes[:, cols].bitcast(FP8X4),
                    rhs_scale=x_plane[:, cols],
                    start=True,
                    stop=True,
                )
            return bank

        w1_codes = mx_tile([P, R], U32, "w1_codes")
        w1_plane = mx_tile([P, R], U8, "w1_plane")
        w1_low = deal(nc.vector.tensor_copy, w1_raw, 0, "w1_low")
        w1_high = deal(nc.scalar.copy, w1_raw, 1, "w1_high")
        quantize_pair(w1_low, w1_codes, w1_plane, 0)
        tab_picked_plane = gather(tab_plane, U8, "tab_picked_plane")
        quantize_pair(w1_high, w1_codes, w1_plane, 1)
        wor_raw = mx_tile([P, PACK, F], F32, "wor_raw", tag="w1_raw")
        nc.sync.dma_start(out=wor_raw[:], in_=wor.rearrange("(p s) f -> p s f", s=PACK))
        tab_picked = gather(tab_pool, U32, "tab_picked")
        res_sb = mx_tile([P, PACK, J], F32, "res_sb", tag="tab_pool")
        nc.sync.dma_start(out=res_sb[:], in_=res.rearrange("(p t) j -> p t j", t=PACK))
        a_banks = [product(w1_codes, w1_plane, tab_picked, tab_picked_plane, h, "a_bank%d" % h) for h in range(HALVES)]
        dtab_picked_plane = gather(dtab_plane, U8, "dtab_picked_plane")

        def group_sums(bank, order, name, tag=None):
            shape = [P, PACK, GH] if order == "t g" else [P, GH, PACK]
            sums = mx_tile(shape, F32, name, tag)
            nc.vector.tensor_reduce(
                out=sums[:],
                in_=bank[:].rearrange("p t (g i) -> p %s i" % order, i=GROUP),
                axis=AXIS_X,
                op=ALU.add,
            )
            return sums

        a_sums = [group_sums(a_banks[0], "t g", "a_sum0")]
        dtab_picked = gather(dtab_pool, U32, "dtab_picked")
        a_sums.append(group_sums(a_banks[1], "t g", "a_sum1", tag="steep_sb"))
        ta_banks = [
            product(w1_codes, w1_plane, dtab_picked, dtab_picked_plane[DTAB_ROW:P, :], h, "ta_bank%d" % h)
            for h in range(HALVES)
        ]

        ta_factors, sum_factors = [], []
        for h in range(HALVES):
            gate = sb.tile([P, PACK, GH], F32, name="gate%d" % h)
            rest = sb.tile([P, PACK, GH], F32, name="rest%d" % h)
            for t in range(PACK):
                nc.scalar.activation(
                    out=gate[:, t, :],
                    in_=a_sums[h][:, t, :],
                    func=ACT.Sigmoid,
                    bias=bias_sb[:, t : t + 1],
                    scale=mean_steep[:, t : t + 1],
                )
            for t in range(PACK):
                nc.scalar.activation(
                    out=rest[:, t, :],
                    in_=gate[:, t, :],
                    func=ACT.Identity,
                    bias=slope[:, t : t + 1],
                    scale=neg_slope[:, t : t + 1],
                )
            ta_factor = sb.tile([P, GH, PACK], F32, name="ta_factor%d" % h)
            sum_factor = sb.tile([P, GH, PACK], F32, name="sum_factor%d" % h)
            nc.gpsimd.tensor_tensor(
                sum_factor[:], gate[:].rearrange("p t g -> p g t"), rest[:].rearrange("p t g -> p g t"), ALU.mult
            )
            for t in range(PACK):
                nc.scalar.activation(
                    out=ta_factor[:, :, t], in_=gate[:, t, :], func=ACT.Copy, scale=rs_sb[:, t : t + 1]
                )
            ta_factors.append(ta_factor)
            sum_factors.append(sum_factor)

        wor_codes = mx_tile([P, F], U32, "wor_codes")
        wor_plane = mx_tile([P, F], U8, "wor_plane")
        wor_low = deal(nc.scalar.copy, wor_raw, 0, "wor_low")
        wor_high = deal(nc.scalar.copy, wor_raw, 1, "wor_high")

        def times_group_factor(bank, factor, name):
            scaled = sb.tile([P, GH, GROUP, PACK], F32, name=name)
            nc.vector.tensor_tensor(
                scaled[:],
                bank[:].rearrange("p t (g i) -> p g i t", i=GROUP),
                factor.unsqueeze(2).to_broadcast([P, GH, GROUP, PACK]),
                ALU.mult,
            )
            return scaled

        a_factors = []
        for h in range(HALVES):
            ta_sum = group_sums(ta_banks[h], "g t", "ta_sum%d" % h)
            a_factor = sb.tile([P, GH, PACK], F32, name="a_factor%d" % h)
            nc.gpsimd.tensor_tensor(a_factor[:], ta_sum[:], sum_factors[h][:], ALU.mult)
            a_factors.append(a_factor)
        fo_codes = mx_tile([P, J], U32, "fo_codes")
        fo_plane = mx_tile([P, J], U8, "fo_plane")

        def add_terms(engine, ta_term, a_term, name):
            grouped = mx_tile([P, JH * PACK], BF16, name)
            engine.tensor_tensor(
                grouped[:],
                ta_term[:].rearrange("p g i t -> p (g i t)"),
                a_term[:].rearrange("p g i t -> p (g i t)"),
                ALU.add,
            )
            return grouped

        def quantize_half(grouped, codes, plane, half):
            cols = slice(JH * half, JH * (half + 1))
            nc.vector.quantize_mx(out=codes[:, cols].bitcast(FP8X4), scales=plane[:, cols], in_=grouped)

        ta_term0 = times_group_factor(ta_banks[0], ta_factors[0][:], "ta_term0")
        a_term0 = times_group_factor(a_banks[0], a_factors[0][:], "a_term0")
        fo_grouped0 = add_terms(nc.gpsimd, ta_term0, a_term0, "fo_grouped0")
        ta_term1 = times_group_factor(ta_banks[1], ta_factors[1][:], "ta_term1")
        a_term1 = times_group_factor(a_banks[1], a_factors[1][:], "a_term1")
        quantize_pair(wor_low, wor_codes, wor_plane, 0)
        quantize_half(fo_grouped0[:], fo_codes, fo_plane, 0)
        fo_grouped1 = add_terms(nc.vector, ta_term1, a_term1, "fo_grouped1")
        quantize_pair(wor_high, wor_codes, wor_plane, 1)
        quantize_half(fo_grouped1[:], fo_codes, fo_plane, 1)
        yo_banks = [product(wor_codes, wor_plane, fo_codes, fo_plane, h, "yo_bank%d" % h) for h in range(HALVES)]

        y_codes = mx_tile([P, J], U32, "y_codes")
        y_plane = mx_tile([P, J], U8, "y_plane")
        out_rows = out_0.rearrange("(p t) j -> p t j", t=PACK)
        y_grouped = []
        for h in range(HALVES):
            cols = slice(JH * h, JH * (h + 1))
            y = sb.tile([P, PACK, JH], F32, name="y%d" % h)
            nc.vector.tensor_tensor(y[:], yo_banks[h][:], res_sb[:, :, cols], ALU.add)
            nc.sync.dma_start(out=out_rows[:, :, cols], in_=y[:])
            grouped = mx_tile([P, JH, PACK], BF16, "y_grouped%d" % h)
            copy = (nc.scalar.copy, nc.vector.tensor_copy)[h]
            copy(
                out=grouped[:].rearrange("p (c i) t -> p c t i", i=4),
                in_=y[:].rearrange("p t (c i) -> p c t i", i=4),
            )
            y_grouped.append(grouped)
        for h in range(HALVES):
            cols = slice(JH * h, JH * (h + 1))
            nc.vector.quantize_mx(
                out=y_codes[:, cols].bitcast(FP8X4),
                scales=y_plane[:, cols],
                in_=y_grouped[h][:].rearrange("p j t -> p (j t)"),
            )
        nc.sync.dma_start(out=words_view(out_1), in_=y_codes[:].bitcast(I32))
        for q in range(QUADRANTS):
            queue = (nc.scalar, nc.sync)[q % 2]
            queue.dma_start(
                out=out_2[0, PACK * q : PACK * (q + 1), :].bitcast(I32),
                in_=y_plane[32 * q : 32 * q + PACK, :].bitcast(I32),
            )
